import numpy as np
import ml_dtypes


def mxq(x, axis, fmt="e4m3"):
    dtype, down = {"e4m3": (ml_dtypes.float8_e4m3fn, 7), "e5m2": (ml_dtypes.float8_e5m2, 14)}[fmt]
    v = np.moveaxis(np.asarray(x, np.float32).astype(ml_dtypes.bfloat16).astype(np.float64), axis, -1)
    blocks = v.reshape(v.shape[:-1] + (-1, 32))
    amax = np.abs(blocks).max(-1, keepdims=True)
    byte = np.maximum(np.where(amax > 0, np.frexp(amax)[1] - 1 + 127, 0) - down, 1)
    scale = np.exp2(byte - 127.0)
    codes = (blocks / scale).astype(np.float32).astype(dtype).astype(np.float64)
    return np.moveaxis((codes * scale).reshape(v.shape), -1, axis)


WIDE = False


def mx_kscale(k):
    if not WIDE:
        return np.ones(k)
    levels = np.array([10, -10, 5, -5, 0])
    if k % 512:
        return np.exp2(np.random.permutation(np.resize(levels, k // 32))).repeat(32)
    a = np.empty((k // 512, 16))
    for p in range(k // 512):
        a[p, :8] = np.random.permutation(np.resize(levels, 8))
        for g in range(8):
            far = levels[np.abs(levels - a[p, g]) >= 10]
            a[p, g + 8] = far[np.random.randint(len(far))]
    return np.exp2(a.ravel()).repeat(32)


def f64(x):
    return np.asarray(x).astype(np.float64)


def striped(idx):
    return np.tile(idx.reshape(-1, 16).T, (8, 1)).astype(np.uint16)


def unstriped(offs):
    return offs[:16].T.reshape(-1).astype(np.int64)


def striped8(idx):
    return np.concatenate([x.reshape(-1, 16).T for x in idx]).astype(np.uint16)


def runs(offs, k):
    lists = np.stack([offs[16 * r : 16 * r + 16].T.reshape(-1) for r in range(8)]).astype(np.int64)
    return lists[np.arange(k) % 512 // 64]


def pack_weight(w):
    k, n = w.shape
    w = f64(np.asarray(w, np.float32).astype(ml_dtypes.bfloat16)).reshape(k // 32, 32, n)
    amax = np.abs(w).max(1)
    byte = np.clip(np.where(amax > 0, np.frexp(amax)[1] - 1 + 127 - 7, 1), 1, 254)
    scaled = (w * np.exp2(127.0 - byte)[:, None, :]).reshape(k, n).astype(np.float32)
    words = np.ascontiguousarray(scaled.reshape(k // 512, 128, 4, n).transpose(0, 1, 3, 2)).astype(ml_dtypes.float8_e4m3fn).view(np.uint8)
    return words, np.ascontiguousarray(byte.astype(np.uint8).reshape(k // 512, 16, n))


def unpack_weight(words, scales):
    g, p, n, _ = words.shape
    vals = np.ascontiguousarray(words).view(ml_dtypes.float8_e4m3fn).astype(np.float64) * np.repeat(np.exp2(scales.astype(np.float64) - 127.0), 8, axis=1)[..., None]
    return vals.transpose(0, 1, 3, 2).reshape(g * 512, n)

def planes(y):
    n, m = y.shape
    v = y.astype(np.float32).astype(ml_dtypes.bfloat16).astype(np.float64).reshape(n // 32, 32, m)
    top = np.abs(v).max(1)
    byte = np.clip(np.where(top > 0, np.frexp(top)[1] - 1 + 127 - 7, 1), 1, 254)
    codes = (v * np.exp2(127.0 - byte)[:, None, :]).reshape(n, m).astype(np.float32).astype(ml_dtypes.float8_e4m3fn).view(np.uint8)
    words = codes.reshape(n // 512, 128, 4, m).transpose(0, 1, 3, 2)
    return np.ascontiguousarray(words), np.ascontiguousarray(byte.astype(np.uint8).reshape(n // 512, 16, m))


K, T, S, G, H, C = 512, 1024, 512, 2048, 512, 512


def setup_inputs():
    n = np.random.standard_normal
    s = mx_kscale(K)[:, None]
    packed_xT = pack_weight(n((K, T)) * s)
    packed_dT = pack_weight(n((K, G)) / s)
    return {
        "x_words": packed_xT[0],
        "x_scales": packed_xT[1],
        "d_words": packed_dT[0],
        "d_scales": packed_dT[1],
        "gs": (np.random.uniform(0.5, 1.5, (K, 1)) / s).astype(np.float32),
        "offs": striped(np.random.permutation(T)[:S]),
        "k1": striped8(np.random.randint(0, G, (8, H))),
        "n1": striped8(np.stack([np.random.permutation(S) for _ in range(8)])),
        "n2": striped8(np.stack([np.random.permutation(S) for _ in range(8)])),
        "n3": striped8(np.stack([np.random.permutation(S) for _ in range(8)])),
        "cand": striped(np.random.permutation(T)[:C]),
        "two": striped(np.random.permutation(T)[:S]),
        "k2": striped8(np.random.randint(0, G, (8, H))),
        "n4": striped(np.random.permutation(S)),
        "n5": striped(np.random.permutation(S)),
    }


def reference(x_words, x_scales, d_words, d_scales, gs, offs, k1, n1, n2, n3, cand, two, k2, n4, n5):
    x_cand = unpack_weight(x_words, x_scales)[:, unstriped(cand)]
    d_k1 = unpack_weight(d_words, d_scales)[np.arange(K)[:, None], runs(k1, K)]
    xq = unpack_weight(x_words, x_scales)[:, unstriped(offs)]
    h = 0.0625 * (d_k1.T @ xq)
    st = h - (h[np.arange(H)[:, None], runs(n1, H)])
    su = np.maximum(st, st[np.arange(H)[:, None], runs(n2, H)])
    z = f64(gs) * (su + 0.5 * (su[np.arange(H)[:, None], runs(n3, H)]))
    a = 0.0625 * ((x_cand.T @ mxq(z, 0, "e4m3")))
    d_k2 = unpack_weight(d_words, d_scales)[np.arange(K)[:, None], runs(k2, K)]
    x_two = unpack_weight(x_words, x_scales)[:, unstriped(two)]
    b = 0.0625 * (d_k2.T @ x_two)
    out_0 = np.maximum(a, b[:, unstriped(n5)]) - (np.minimum(a[:, unstriped(n4)], b))
    return (out_0,) + planes(out_0)

@@ -1,0 +1,200 @@
+from contextlib import ExitStack
+
+import concourse.mybir as mybir
+
+F32 = mybir.dt.float32
+BF16 = mybir.dt.bfloat16
+I32 = mybir.dt.int32
+U32 = mybir.dt.uint32
+U16 = mybir.dt.uint16
+U8 = mybir.dt.uint8
+FP8X4 = mybir.dt.float8_e4m3fn_x4
+ALU = mybir.AluOpType
+COPY = mybir.ActivationFunctionType.Copy
+
+P = 128
+PACK = 4
+N = 512
+TOKENS = 1024
+CODEWORDS = 2048
+WIDE = 1024
+WIDE_ONE = 704
+SIXTEENTH = 0.0625
+FLOPS = 3 * 2 * 512 * 512 * 512
+
+
+def tile_picked_pqcjmaxbthree_none_po_kernel(
+    tc, x_words, x_scales, d_words, d_scales, gs, offs, k1, n1, n2, n3, cand, two, k2, n4, n5, out_0, out_1, out_2
+):
+    nc = tc.nc
+    with ExitStack() as ctx:
+        keep = ctx.enter_context(tc.tile_pool(name="keep", bufs=1))
+        psum = ctx.enter_context(tc.psum_pool(name="psum", bufs=1))
+
+        def new(shape, dtype, name):
+            return keep.tile(shape, dtype, name=name, align_bytes=64)
+
+        def load_list(src, name):
+            t = keep.tile([P, N // 16], U16, name=name)
+            nc.sync.dma_start(t[:], src)
+            return t
+
+        ds = new([P, CODEWORDS], U8, "ds")
+        xs = new([P, TOKENS], U8, "xs")
+        dw = new([P, CODEWORDS], U32, "dw")
+        xw = new([P, TOKENS], U32, "xw")
+        win = [new([P, WIDE], F32, "win%d" % t) for t in range(PACK)]
+        winb = [new([P, WIDE_ONE], F32, "winb%d" % t) for t in range(PACK)]
+        for t in range(PACK):
+            nc.vector.memset(win[t][:, N:], 0.0)
+            nc.vector.memset(winb[t][:, N:], 0.0)
+
+        l_k1 = load_list(k1, "l_k1")
+        nc.sync.dma_start(
+            ds[:].bitcast(I32), d_scales[0].bitcast(I32).unsqueeze(1).to_broadcast([16, 8, CODEWORDS // 4])
+        )
+        nc.sync.dma_start(xw[:].bitcast(I32), x_words[0].rearrange("p n t -> p (n t)").bitcast(I32))
+        l_offs = load_list(offs, "l_offs")
+        nc.sync.dma_start(dw[:].bitcast(I32), d_words[0].rearrange("p n t -> p (n t)").bitcast(I32))
+        for i in range(PACK):
+            nc.sync.dma_start(
+                xs[i:P:4, :].bitcast(I32),
+                x_scales[0][i:16:4, :].bitcast(I32).unsqueeze(1).to_broadcast([4, 8, TOKENS // 4]),
+            )
+        l_k2 = load_list(k2, "l_k2")
+        l_n1 = load_list(n1, "l_n1")
+        l_two = load_list(two, "l_two")
+        l_cand = load_list(cand, "l_cand")
+        l_n2 = load_list(n2, "l_n2")
+        l_n3 = load_list(n3, "l_n3")
+        l_n5 = load_list(n5, "l_n5")
+        l_n4 = load_list(n4, "l_n4")
+        gain = new([P, PACK], F32, "gain")
+        nc.sync.dma_start(gain[:], gs.rearrange("(p t) o -> p (t o)", t=PACK))
+        half_gain = new([P, PACK], F32, "half_gain")
+
+        def gather(table, lst, dtype, name):
+            g = new([P, N], dtype, name)
+            nc.vector.tensor_copy(out=g[:], in_=table[:].indirect(lst[:]))
+            return g
+
+        def deal(src, dtype, name):
+            d = new([P, N], dtype, name)
+            nc.vector.tensor_copy(
+                out=d[:].rearrange("p (t m) -> p t m", t=PACK), in_=src[:].rearrange("p (m t) -> p t m", t=PACK)
+            )
+            return d
+
+        def code_scales(lst, name, queue):
+            d = deal(gather(ds, lst, U8, name + "_gb"), U8, name + "_db")
+            for i in range(1, PACK):
+                queue.dma_start(d[i:P:32, :].bitcast(I32), d[8 * i : P : 32, :].bitcast(I32))
+            return d
+
+        def product(tag, lw, ls, rw, rs):
+            banks = []
+            for t in range(PACK):
+                bank = psum.tile([P, N], F32, name="%s%d" % (tag, t), tag="%s%d" % (tag, t))
+                cols = slice(t * P, (t + 1) * P)
+                nc.tensor.matmul_mx(
+                    out=bank[:], lhsT=lw[:, cols].bitcast(FP8X4), lhsT_scale=ls[:, cols],
+                    rhs=rw[:].bitcast(FP8X4), rhs_scale=rs[:], start=True, stop=True,
+                )
+                banks.append(bank)
+            return banks
+
+        def fetch(window, lst, name, on_vector=False):
+            g = new([P, N], F32, name)
+            if on_vector:
+                nc.vector.tensor_copy(out=g[:], in_=window[:].indirect(lst[:]))
+            else:
+                nc.scalar.activation(out=g[:], in_=window[:].indirect(lst[:]), func=COPY)
+            return g
+
+        def quantise(src, words, scales, name, shares):
+            rounded = new([P, N, PACK], BF16, name)
+            half = N // 2
+            for copy, cols in shares:
+                copy(
+                    out=rounded[:, cols, :].rearrange("p (c i) t -> p c t i", i=4),
+                    in_=src[:, :, cols].rearrange("p t (c i) -> p c t i", i=4),
+                )
+            for c in range(2):
+                cols = slice(c * half, (c + 1) * half)
+                nc.vector.quantize_mx(
+                    out=words[:, cols].bitcast(FP8X4), scales=scales[:, cols],
+                    in_=rounded[:, cols, :].rearrange("p c t -> p (c t)"),
+                )
+
+        k1_s = code_scales(l_k1, "k1", nc.scalar)
+        offs_w = gather(xw, l_offs, U32, "offs_w")
+        k1_w = deal(gather(dw, l_k1, U32, "k1_gw"), U32, "k1_w")
+        offs_s = gather(xs, l_offs, U8, "offs_s")
+        h = product("h", k1_w, k1_s, offs_w, offs_s)
+
+        k2_s = code_scales(l_k2, "k2", nc.sync)
+        k2_w = deal(gather(dw, l_k2, U32, "k2_gw"), U32, "k2_w")
+        two_w = gather(xw, l_two, U32, "two_w")
+        two_s = gather(xs, l_two, U8, "two_s")
+        b = product("b", k2_w, k2_s, two_w, two_s)
+        nc.vector.tensor_scalar(out=half_gain[:], in0=gain[:], scalar1=0.5, scalar2=None, op0=ALU.mult)
+
+        g1 = []
+        for t in range(PACK):
+            nc.scalar.activation(out=win[t][:, :N], in_=h[t][:], func=COPY, scale=SIXTEENTH)
+            g1.append(fetch(win[t], l_n1, "g1_%d" % t))
+        for t in range(PACK):
+            nc.vector.scalar_tensor_tensor(
+                out=win[t][:, :N], in0=h[t][:], scalar=SIXTEENTH, in1=g1[t][:], op0=ALU.mult, op1=ALU.subtract
+            )
+        cand_w = deal(gather(xw, l_cand, U32, "cand_gw"), U32, "cand_w")
+        cand_s = deal(gather(xs, l_cand, U8, "cand_gs"), U8, "cand_s")
+        g2 = [fetch(win[t], l_n2, "g2_%d" % t) for t in range(PACK)]
+        for t in range(PACK):
+            nc.vector.tensor_tensor(out=win[t][:, :N], in0=win[t][:, :N], in1=g2[t][:], op=ALU.max)
+        z = new([P, PACK, N], F32, "z")
+        g3 = [winb[t][:, :N] for t in range(PACK)]
+        for t in range(PACK):
+            nc.scalar.activation(out=g3[t], in_=win[t][:].indirect(l_n3[:]), func=COPY)
+        for t in range(PACK):
+            nc.vector.tensor_scalar(
+                out=z[:, t, :], in0=win[t][:, :N], scalar1=gain[:, t : t + 1], scalar2=None, op0=ALU.mult
+            )
+        for t in range(PACK):
+            nc.vector.scalar_tensor_tensor(
+                out=z[:, t, :], in0=g3[t], scalar=half_gain[:, t : t + 1], in1=z[:, t, :], op0=ALU.mult, op1=ALU.add
+            )
+        z_w = new([P, N], U32, "z_w")
+        z_s = new([P, N], U8, "z_s")
+        quantise(z, z_w, z_s, "z_rounded", [(nc.vector.tensor_copy, slice(0, 256)), (nc.vector.tensor_copy, slice(256, N))])
+        a = product("h", cand_w, cand_s, z_w, z_s)
+
+        g5 = []
+        for t in range(PACK):
+            nc.scalar.activation(out=winb[t][:, :N], in_=b[t][:], func=COPY, scale=SIXTEENTH)
+            g5.append(fetch(winb[t], l_n5, "g5_%d" % t, t >= 2))
+
+        y = new([P, PACK, N], F32, "y")
+        out_rows = out_0.rearrange("(p t) c -> p t c", t=PACK)
+        for t in range(PACK):
+            nc.scalar.activation(out=win[t][:, :N], in_=a[t][:], func=COPY, scale=SIXTEENTH)
+            g4 = fetch(win[t], l_n4, "g4_%d" % t)
+            nc.vector.scalar_tensor_tensor(
+                out=g5[t][:], in0=a[t][:], scalar=SIXTEENTH, in1=g5[t][:], op0=ALU.mult, op1=ALU.max
+            )
+            nc.vector.scalar_tensor_tensor(
+                out=g4[:], in0=b[t][:], scalar=SIXTEENTH, in1=g4[:], op0=ALU.mult, op1=ALU.min
+            )
+            nc.vector.tensor_tensor(out=y[:, t, :], in0=g5[t][:], in1=g4[:], op=ALU.subtract)
+            nc.sync.dma_start(out_rows[:, t, :], y[:, t, :])
+        y_w = new([P, N], U32, "y_w")
+        y_s = new([P, N], U8, "y_s")
+        quantise(
+            y, y_w, y_s, "y_rounded",
+            [(nc.vector.tensor_copy, slice(0, 256)), (nc.vector.tensor_copy, slice(256, 352)), (nc.scalar.copy, slice(352, N))],
+        )
+        out_words = out_1[0].rearrange("p n t -> p (n t)").bitcast(I32)
+        for c in range(2):
+            nc.sync.dma_start(out_words[:, c * 256 : (c + 1) * 256], y_w[:, c * 256 : (c + 1) * 256].bitcast(I32))
+        for i in range(PACK):
+            nc.scalar.dma_start(out_2[0][i:16:4, :].bitcast(I32), y_s[i:P:32, :].bitcast(I32))

@@ -31,8 +31,8 @@ def tile_picked_pqcjmaxbthree_none_po_kernel(
         keep = ctx.enter_context(tc.tile_pool(name="keep", bufs=1))
         psum = ctx.enter_context(tc.psum_pool(name="psum", bufs=1))
 
-        def new(shape, dtype, name):
-            return keep.tile(shape, dtype, name=name, align_bytes=64)
+        def new(shape, dtype, name, tag=None):
+            return keep.tile(shape, dtype, name=name, tag=tag or name, align_bytes=64)
 
         def load_list(src, name):
             t = keep.tile([P, N // 16], U16, name=name)
@@ -45,156 +45,198 @@ def tile_picked_pqcjmaxbthree_none_po_kernel(
         xw = new([P, TOKENS], U32, "xw")
         win = [new([P, WIDE], F32, "win%d" % t) for t in range(PACK)]
         winb = [new([P, WIDE_ONE], F32, "winb%d" % t) for t in range(PACK)]
-        for t in range(PACK):
-            nc.vector.memset(win[t][:, N:], 0.0)
-            nc.vector.memset(winb[t][:, N:], 0.0)
-
+        gain = new([P, PACK], F32, "gain")
+        nc.gpsimd.memset(xs[:].bitcast(I32), 0)
         l_k1 = load_list(k1, "l_k1")
         nc.sync.dma_start(
             ds[:].bitcast(I32), d_scales[0].bitcast(I32).unsqueeze(1).to_broadcast([16, 8, CODEWORDS // 4])
         )
         nc.sync.dma_start(xw[:].bitcast(I32), x_words[0].rearrange("p n t -> p (n t)").bitcast(I32))
         l_offs = load_list(offs, "l_offs")
-        nc.sync.dma_start(dw[:].bitcast(I32), d_words[0].rearrange("p n t -> p (n t)").bitcast(I32))
         for i in range(PACK):
-            nc.sync.dma_start(
-                xs[i:P:4, :].bitcast(I32),
-                x_scales[0][i:16:4, :].bitcast(I32).unsqueeze(1).to_broadcast([4, 8, TOKENS // 4]),
-            )
+            nc.sync.dma_start(xs[i:P:32, :].bitcast(I32), x_scales[0][i:16:4, :].bitcast(I32))
+        nc.sync.dma_start(dw[:].bitcast(I32), d_words[0].rearrange("p n t -> p (n t)").bitcast(I32))
         l_k2 = load_list(k2, "l_k2")
         l_n1 = load_list(n1, "l_n1")
         l_two = load_list(two, "l_two")
-        l_cand = load_list(cand, "l_cand")
         l_n2 = load_list(n2, "l_n2")
+        l_cand = load_list(cand, "l_cand")
         l_n3 = load_list(n3, "l_n3")
         l_n5 = load_list(n5, "l_n5")
         l_n4 = load_list(n4, "l_n4")
-        gain = new([P, PACK], F32, "gain")
         nc.sync.dma_start(gain[:], gs.rearrange("(p t) o -> p (t o)", t=PACK))
-        half_gain = new([P, PACK], F32, "half_gain")
+        for t in range(PACK):
+            nc.vector.memset(win[t][:, N:], 0.0)
+            nc.vector.memset(winb[t][:, N:], 0.0)
 
-        def gather(table, lst, dtype, name):
-            g = new([P, N], dtype, name)
+        def gather(table, lst, dtype, name, tag=None):
+            g = new([P, N], dtype, name, tag)
             nc.vector.tensor_copy(out=g[:], in_=table[:].indirect(lst[:]))
             return g
 
         def deal(src, dtype, name):
             d = new([P, N], dtype, name)
             nc.vector.tensor_copy(
+                out=d[:].rearrange("p (t c i) -> p c t i", t=PACK, i=4),
+                in_=src[:].rearrange("p (c i t) -> p c t i", t=PACK, i=4),
+            )
+            return d
+
+        def deal_bytes(src, name):
+            d = new([P, N], U8, name)
+            nc.vector.tensor_copy(
                 out=d[:].rearrange("p (t m) -> p t m", t=PACK), in_=src[:].rearrange("p (m t) -> p t m", t=PACK)
             )
             return d
 
-        def code_scales(lst, name, queue):
-            d = deal(gather(ds, lst, U8, name + "_gb"), U8, name + "_db")
+        def code_scales(lst, name, queue, tag=None):
+            d = deal_bytes(gather(ds, lst, U8, name + "_gb", tag), name + "_db")
             for i in range(1, PACK):
                 queue.dma_start(d[i:P:32, :].bitcast(I32), d[8 * i : P : 32, :].bitcast(I32))
             return d
 
-        def product(tag, lw, ls, rw, rs):
-            banks = []
+        def product(tag, lw, ls, rw, rs, width):
+            banks = [psum.tile([P, N], F32, name="%s%d" % (tag, t), tag="%s%d" % (tag, t)) for t in range(PACK)]
             for t in range(PACK):
-                bank = psum.tile([P, N], F32, name="%s%d" % (tag, t), tag="%s%d" % (tag, t))
-                cols = slice(t * P, (t + 1) * P)
-                nc.tensor.matmul_mx(
-                    out=bank[:], lhsT=lw[:, cols].bitcast(FP8X4), lhsT_scale=ls[:, cols],
-                    rhs=rw[:].bitcast(FP8X4), rhs_scale=rs[:], start=True, stop=True,
-                )
-                banks.append(bank)
+                rows = slice(t * P, (t + 1) * P)
+                for c in range(0, N, width):
+                    cols = slice(c, c + width)
+                    nc.tensor.matmul_mx(
+                        out=banks[t][:, cols], lhsT=lw[:, rows].bitcast(FP8X4), lhsT_scale=ls[:, rows],
+                        rhs=rw[:, cols].bitcast(FP8X4), rhs_scale=rs[:, cols], start=True, stop=True,
+                    )
             return banks
 
-        def fetch(window, lst, name, on_vector=False):
-            g = new([P, N], F32, name)
+        def fetch(out, window, lst, on_vector, lo=0, hi=N):
+            picked = window[:].indirect(lst[:, lo // 16 : hi // 16])
             if on_vector:
-                nc.vector.tensor_copy(out=g[:], in_=window[:].indirect(lst[:]))
+                nc.vector.tensor_copy(out=out[:, lo:hi], in_=picked)
             else:
-                nc.scalar.activation(out=g[:], in_=window[:].indirect(lst[:]), func=COPY)
-            return g
+                nc.scalar.activation(out=out[:, lo:hi], in_=picked, func=COPY)
 
-        def quantise(src, words, scales, name, shares):
-            rounded = new([P, N, PACK], BF16, name)
-            half = N // 2
-            for copy, cols in shares:
-                copy(
-                    out=rounded[:, cols, :].rearrange("p (c i) t -> p c t i", i=4),
-                    in_=src[:, :, cols].rearrange("p t (c i) -> p c t i", i=4),
-                )
-            for c in range(2):
-                cols = slice(c * half, (c + 1) * half)
-                nc.vector.quantize_mx(
-                    out=words[:, cols].bitcast(FP8X4), scales=scales[:, cols],
-                    in_=rounded[:, cols, :].rearrange("p c t -> p (c t)"),
-                )
+        def weave(copy, rounded, src, cols):
+            copy(
+                out=rounded[:, cols, :].rearrange("p (c i) t -> p c t i", i=4),
+                in_=src[:, :, cols].rearrange("p t (c i) -> p c t i", i=4),
+            )
+
+        def quantise(rounded, words, scales, cols):
+            nc.vector.quantize_mx(
+                out=words[:, cols].bitcast(FP8X4), scales=scales[:, cols],
+                in_=rounded[:, cols, :].rearrange("p c t -> p (c t)"),
+            )
+
+        halves = [slice(0, N // 2), slice(N // 2, N)]
 
         k1_s = code_scales(l_k1, "k1", nc.scalar)
         offs_w = gather(xw, l_offs, U32, "offs_w")
-        k1_w = deal(gather(dw, l_k1, U32, "k1_gw"), U32, "k1_w")
         offs_s = gather(xs, l_offs, U8, "offs_s")
-        h = product("h", k1_w, k1_s, offs_w, offs_s)
+        k1_w = deal(gather(dw, l_k1, U32, "k1_gw"), U32, "k1_w")
+        h = product("h", k1_w, k1_s, offs_w, offs_s, N)
 
-        k2_s = code_scales(l_k2, "k2", nc.sync)
-        k2_w = deal(gather(dw, l_k2, U32, "k2_gw"), U32, "k2_w")
-        two_w = gather(xw, l_two, U32, "two_w")
-        two_s = gather(xs, l_two, U8, "two_s")
-        b = product("b", k2_w, k2_s, two_w, two_s)
-        nc.vector.tensor_scalar(out=half_gain[:], in0=gain[:], scalar1=0.5, scalar2=None, op0=ALU.mult)
+        got = {}
+        picks = {
+            "k2_s": lambda tag: code_scales(l_k2, "k2", nc.sync, tag),
+            "k2_w": lambda tag: deal(gather(dw, l_k2, U32, "k2_gw", tag), U32, "k2_w"),
+            "two_w": lambda tag: gather(xw, l_two, U32, "two_w", tag),
+            "two_s": lambda tag: gather(xs, l_two, U8, "two_s", tag),
+            "cand_w": lambda tag: deal(gather(xw, l_cand, U32, "cand_gw", tag), U32, "cand_w"),
+            "cand_s": lambda tag: deal_bytes(gather(xs, l_cand, U8, "cand_gs", tag), "cand_s"),
+        }
+        behind = {"g1_0":"two_w","g1_1":"two_s","g1_2":"cand_w","g1_3":"cand_s"}
 
-        g1 = []
+        def pick(tag):
+            if tag in behind:
+                got[behind[tag]] = picks[behind[tag]](tag)
+
+        for name in picks:
+            if name not in behind.values():
+                got[name] = picks[name]("k1_gw")
+        g1 = [new([P, N], F32, "g1_%d" % t) for t in range(PACK)]
         for t in range(PACK):
             nc.scalar.activation(out=win[t][:, :N], in_=h[t][:], func=COPY, scale=SIXTEENTH)
-            g1.append(fetch(win[t], l_n1, "g1_%d" % t))
+            fetch(g1[t], win[t], l_n1, t in ())
         for t in range(PACK):
             nc.vector.scalar_tensor_tensor(
                 out=win[t][:, :N], in0=h[t][:], scalar=SIXTEENTH, in1=g1[t][:], op0=ALU.mult, op1=ALU.subtract
             )
-        cand_w = deal(gather(xw, l_cand, U32, "cand_gw"), U32, "cand_w")
-        cand_s = deal(gather(xs, l_cand, U8, "cand_gs"), U8, "cand_s")
-        g2 = [fetch(win[t], l_n2, "g2_%d" % t) for t in range(PACK)]
+            pick("g1_%d" % t)
+        g2 = [new([P, N], F32, "g2_%d" % t) for t in range(PACK)]
         for t in range(PACK):
+            fetch(g2[t], win[t], l_n2, t in ())
             nc.vector.tensor_tensor(out=win[t][:, :N], in0=win[t][:, :N], in1=g2[t][:], op=ALU.max)
+            pick("g2_%d" % t)
         z = new([P, PACK, N], F32, "z")
         g3 = [winb[t][:, :N] for t in range(PACK)]
+        z_rounded = new([P, N, PACK], BF16, "z_rounded")
+        half_gain = new([P, PACK], F32, "half_gain")
+        nc.vector.tensor_scalar(out=half_gain[:], in0=gain[:], scalar1=0.5, scalar2=None, op0=ALU.mult)
         for t in range(PACK):
-            nc.scalar.activation(out=g3[t], in_=win[t][:].indirect(l_n3[:]), func=COPY)
-        for t in range(PACK):
+            fetch(g3[t], win[t], l_n3, t in ())
             nc.vector.tensor_scalar(
                 out=z[:, t, :], in0=win[t][:, :N], scalar1=gain[:, t : t + 1], scalar2=None, op0=ALU.mult
             )
-        for t in range(PACK):
             nc.vector.scalar_tensor_tensor(
-                out=z[:, t, :], in0=g3[t], scalar=half_gain[:, t : t + 1], in1=z[:, t, :], op0=ALU.mult, op1=ALU.add
+                out=z[:, t, :], in0=g3[t][:], scalar=half_gain[:, t : t + 1], in1=z[:, t, :], op0=ALU.mult, op1=ALU.add
             )
+        for cols in halves:
+            weave(nc.vector.tensor_copy, z_rounded, z, cols)
         z_w = new([P, N], U32, "z_w")
         z_s = new([P, N], U8, "z_s")
-        quantise(z, z_w, z_s, "z_rounded", [(nc.vector.tensor_copy, slice(0, 256)), (nc.vector.tensor_copy, slice(256, N))])
-        a = product("h", cand_w, cand_s, z_w, z_s)
+        for cols in halves:
+            quantise(z_rounded, z_w, z_s, cols)
 
-        g5 = []
-        for t in range(PACK):
-            nc.scalar.activation(out=winb[t][:, :N], in_=b[t][:], func=COPY, scale=SIXTEENTH)
-            g5.append(fetch(winb[t], l_n5, "g5_%d" % t, t >= 2))
+        b = product("b", got["k2_w"], got["k2_s"], got["two_w"], got["two_s"], N)
+        a = product("h", got["cand_w"], got["cand_s"], z_w, z_s, N)
 
         y = new([P, PACK, N], F32, "y")
+        y_rounded = new([P, N, PACK], BF16, "y_rounded")
+        y_w = new([P, N], U32, "y_w")
+        y_s = new([P, N], U8, "y_s")
         out_rows = out_0.rearrange("(p t) c -> p t c", t=PACK)
-        for t in range(PACK):
-            nc.scalar.activation(out=win[t][:, :N], in_=a[t][:], func=COPY, scale=SIXTEENTH)
-            g4 = fetch(win[t], l_n4, "g4_%d" % t)
+        out_words = out_1[0].rearrange("p n t -> p (n t)").bitcast(I32)
+        g4 = [new([P, N], F32, "g4_%d" % t) for t in range(PACK)]
+        g5 = [new([P, N], F32, "g5_%d" % t) for t in range(PACK)]
+
+        def leave(t, dst, bank, on_vector):
+            if on_vector:
+                nc.vector.tensor_scalar(out=dst[:, :N], in0=bank[:], scalar1=SIXTEENTH, scalar2=None, op0=ALU.mult)
+            else:
+                nc.scalar.activation(out=dst[:, :N], in_=bank[:], func=COPY, scale=SIXTEENTH)
+
+        def finish(t, cols):
+            nc.vector.scalar_tensor_tensor(
+                out=g4[t][:, cols], in0=b[t][:, cols], scalar=SIXTEENTH, in1=g4[t][:, cols], op0=ALU.mult, op1=ALU.min
+            )
+            eng = nc.gpsimd if t in () else nc.vector
+            eng.tensor_tensor(out=y[:, t, cols], in0=g5[t][:, cols], in1=g4[t][:, cols], op=ALU.subtract)
+
+        def larger(t):
             nc.vector.scalar_tensor_tensor(
                 out=g5[t][:], in0=a[t][:], scalar=SIXTEENTH, in1=g5[t][:], op0=ALU.mult, op1=ALU.max
             )
-            nc.vector.scalar_tensor_tensor(
-                out=g4[:], in0=b[t][:], scalar=SIXTEENTH, in1=g4[:], op0=ALU.mult, op1=ALU.min
-            )
-            nc.vector.tensor_tensor(out=y[:, t, :], in0=g5[t][:], in1=g4[:], op=ALU.subtract)
-            nc.sync.dma_start(out_rows[:, t, :], y[:, t, :])
-        y_w = new([P, N], U32, "y_w")
-        y_s = new([P, N], U8, "y_s")
-        quantise(
-            y, y_w, y_s, "y_rounded",
-            [(nc.vector.tensor_copy, slice(0, 256)), (nc.vector.tensor_copy, slice(256, 352)), (nc.scalar.copy, slice(352, N))],
-        )
-        out_words = out_1[0].rearrange("p n t -> p (n t)").bitcast(I32)
-        for c in range(2):
-            nc.sync.dma_start(out_words[:, c * 256 : (c + 1) * 256], y_w[:, c * 256 : (c + 1) * 256].bitcast(I32))
+
+        for t in range(PACK):
+            leave(t, winb[t], b[t], t in (3,))
+            fetch(g5[t], winb[t], l_n5, t in (3,))
+        split = ()
+        for t in range(PACK):
+            leave(t, win[t], a[t], t in (0,1))
+            larger(t)
+            if t not in split:
+                fetch(g4[t], win[t], l_n4, t in ())
+                finish(t, slice(0, N))
+                nc.sync.dma_start(out_rows[:, t, :], y[:, t, :])
+        for c, cols in enumerate(halves):
+            for t in split:
+                fetch(g4[t], win[t], l_n4, False, cols.start, cols.stop)
+                finish(t, cols)
+                nc.sync.dma_start(out_rows[:, t, cols], y[:, t, cols])
+            cut = cols.stop - (0, 160)[c]
+            weave(nc.vector.tensor_copy, y_rounded, y, slice(cols.start, cut))
+            if cut < cols.stop:
+                weave(nc.scalar.copy, y_rounded, y, slice(cut, cols.stop))
+            quantise(y_rounded, y_w, y_s, cols)
+            nc.sync.dma_start(out_words[:, cols], y_w[:, cols].bitcast(I32))
         for i in range(PACK):
             nc.scalar.dma_start(out_2[0][i:16:4, :].bitcast(I32), y_s[i:P:32, :].bitcast(I32))

@@ -46,22 +46,22 @@ def tile_picked_pqcjmaxbthree_none_po_kernel(
         win = [new([P, WIDE], F32, "win%d" % t) for t in range(PACK)]
         winb = [new([P, WIDE_ONE], F32, "winb%d" % t) for t in range(PACK)]
         gain = new([P, PACK], F32, "gain")
-        nc.gpsimd.memset(xs[:].bitcast(I32), 0)
+        nc.gpsimd.memset(ds[:].bitcast(I32), 0)
+        nc.vector.memset(xs[:].bitcast(I32), 0)
+        nc.scalar.dma_start(ds[0:P:8, :].bitcast(I32), d_scales[0].bitcast(I32))
         l_k1 = load_list(k1, "l_k1")
-        nc.sync.dma_start(
-            ds[:].bitcast(I32), d_scales[0].bitcast(I32).unsqueeze(1).to_broadcast([16, 8, CODEWORDS // 4])
-        )
         nc.sync.dma_start(xw[:].bitcast(I32), x_words[0].rearrange("p n t -> p (n t)").bitcast(I32))
         l_offs = load_list(offs, "l_offs")
         for i in range(PACK):
+            if i == PACK - 1:
+                nc.sync.dma_start(dw[:].bitcast(I32), d_words[0].rearrange("p n t -> p (n t)").bitcast(I32))
             nc.sync.dma_start(xs[i:P:32, :].bitcast(I32), x_scales[0][i:16:4, :].bitcast(I32))
-        nc.sync.dma_start(dw[:].bitcast(I32), d_words[0].rearrange("p n t -> p (n t)").bitcast(I32))
-        l_k2 = load_list(k2, "l_k2")
         l_n1 = load_list(n1, "l_n1")
-        l_two = load_list(two, "l_two")
         l_n2 = load_list(n2, "l_n2")
-        l_cand = load_list(cand, "l_cand")
         l_n3 = load_list(n3, "l_n3")
+        l_k2 = load_list(k2, "l_k2")
+        l_two = load_list(two, "l_two")
+        l_cand = load_list(cand, "l_cand")
         l_n5 = load_list(n5, "l_n5")
         l_n4 = load_list(n4, "l_n4")
         nc.sync.dma_start(gain[:], gs.rearrange("(p t) o -> p (t o)", t=PACK))
@@ -151,7 +151,7 @@ def tile_picked_pqcjmaxbthree_none_po_kernel(
 
         for name in picks:
             if name not in behind.values():
-                got[name] = picks[name]("k1_gw")
+                got[name] = picks[name](None)
         g1 = [new([P, N], F32, "g1_%d" % t) for t in range(PACK)]
         for t in range(PACK):
             nc.scalar.activation(out=win[t][:, :N], in_=h[t][:], func=COPY, scale=SIXTEENTH)
@@ -176,9 +176,11 @@ def tile_picked_pqcjmaxbthree_none_po_kernel(
             nc.vector.tensor_scalar(
                 out=z[:, t, :], in0=win[t][:, :N], scalar1=gain[:, t : t + 1], scalar2=None, op0=ALU.mult
             )
-            nc.vector.scalar_tensor_tensor(
-                out=z[:, t, :], in0=g3[t][:], scalar=half_gain[:, t : t + 1], in1=z[:, t, :], op0=ALU.mult, op1=ALU.add
-            )
+            for cols in halves if t == PACK - 1 else [slice(0, N)]:
+                nc.vector.scalar_tensor_tensor(
+                    out=z[:, t, cols], in0=g3[t][:, cols], scalar=half_gain[:, t : t + 1], in1=z[:, t, cols],
+                    op0=ALU.mult, op1=ALU.add,
+                )
         for cols in halves:
             weave(nc.vector.tensor_copy, z_rounded, z, cols)
         z_w = new([P, N], U32, "z_w")
@@ -204,11 +206,13 @@ def tile_picked_pqcjmaxbthree_none_po_kernel(
             else:
                 nc.scalar.activation(out=dst[:, :N], in_=bank[:], func=COPY, scale=SIXTEENTH)
 
-        def finish(t, cols):
+        def smaller(t, cols):
             nc.vector.scalar_tensor_tensor(
                 out=g4[t][:, cols], in0=b[t][:, cols], scalar=SIXTEENTH, in1=g4[t][:, cols], op0=ALU.mult, op1=ALU.min
             )
-            eng = nc.gpsimd if t in () else nc.vector
+
+        def finish(t, cols):
+            eng = nc.gpsimd if t in (0,1,2) else nc.vector
             eng.tensor_tensor(out=y[:, t, cols], in0=g5[t][:, cols], in1=g4[t][:, cols], op=ALU.subtract)
 
         def larger(t):
@@ -218,14 +222,21 @@ def tile_picked_pqcjmaxbthree_none_po_kernel(
 
         for t in range(PACK):
             leave(t, winb[t], b[t], t in (3,))
-            fetch(g5[t], winb[t], l_n5, t in (3,))
+            if t < PACK - 1:
+                fetch(g5[t], winb[t], l_n5, False)
         split = ()
         for t in range(PACK):
-            leave(t, win[t], a[t], t in (0,1))
-            larger(t)
+            if t == 1:
+                fetch(g5[PACK - 1], winb[PACK - 1], l_n5, True)
+            leave(t, win[t], a[t], t in (0,))
             if t not in split:
-                fetch(g4[t], win[t], l_n4, t in ())
-                finish(t, slice(0, N))
+                fetch(g4[t], win[t], l_n4, t in (0,))
+                larger(t)
+                parts = halves if t == PACK - 1 else [slice(0, N)]
+                for cols in parts:
+                    smaller(t, cols)
+                for cols in parts:
+                    finish(t, cols)
                 nc.sync.dma_start(out_rows[:, t, :], y[:, t, :])
         for c, cols in enumerate(halves):
             for t in split:

@@ -74,16 +74,16 @@ def tile_picked_pqcjmaxbthree_none_po_kernel(
             nc.vector.tensor_copy(out=g[:], in_=table[:].indirect(lst[:]))
             return g
 
-        def deal(src, dtype, name):
-            d = new([P, N], dtype, name)
+        def deal(src, dtype, name, tag=None):
+            d = new([P, N], dtype, name, tag)
             nc.vector.tensor_copy(
                 out=d[:].rearrange("p (t c i) -> p c t i", t=PACK, i=4),
                 in_=src[:].rearrange("p (c i t) -> p c t i", t=PACK, i=4),
             )
             return d
 
-        def deal_bytes(src, name):
-            d = new([P, N], U8, name)
+        def deal_bytes(src, name, tag=None):
+            d = new([P, N], U8, name, tag)
             nc.vector.tensor_copy(
                 out=d[:].rearrange("p (t m) -> p t m", t=PACK), in_=src[:].rearrange("p (m t) -> p t m", t=PACK)
             )
@@ -135,44 +135,33 @@ def tile_picked_pqcjmaxbthree_none_po_kernel(
         h = product("h", k1_w, k1_s, offs_w, offs_s, N)
 
         got = {}
-        picks = {
-            "k2_s": lambda tag: code_scales(l_k2, "k2", nc.sync, tag),
-            "k2_w": lambda tag: deal(gather(dw, l_k2, U32, "k2_gw", tag), U32, "k2_w"),
-            "two_w": lambda tag: gather(xw, l_two, U32, "two_w", tag),
-            "two_s": lambda tag: gather(xs, l_two, U8, "two_s", tag),
-            "cand_w": lambda tag: deal(gather(xw, l_cand, U32, "cand_gw", tag), U32, "cand_w"),
-            "cand_s": lambda tag: deal_bytes(gather(xs, l_cand, U8, "cand_gs", tag), "cand_s"),
-        }
-        behind = {"g1_0":"two_w","g1_1":"two_s","g1_2":"cand_w","g1_3":"cand_s"}
-
-        def pick(tag):
-            if tag in behind:
-                got[behind[tag]] = picks[behind[tag]](tag)
-
-        for name in picks:
-            if name not in behind.values():
-                got[name] = picks[name](None)
+        got["k2_s"] = code_scales(l_k2, "k2", nc.sync)
+        got["k2_w"] = deal(gather(dw, l_k2, U32, "k2_gw"), U32, "k2_w")
+        got["two_w"] = gather(xw, l_two, U32, "two_w")
+        got["two_s"] = gather(xs, l_two, U8, "two_s")
+        cand_gw = gather(xw, l_cand, U32, "cand_gw")
+        cand_gs = gather(xs, l_cand, U8, "cand_gs")
+        half_gain = new([P, PACK], F32, "half_gain")
+        nc.gpsimd.tensor_scalar(out=half_gain[:], in0=gain[:], scalar1=0.5, scalar2=0.0, op0=ALU.mult, op1=ALU.add)
         g1 = [new([P, N], F32, "g1_%d" % t) for t in range(PACK)]
+        g1[2] = winb[0][:, :N]
         for t in range(PACK):
             nc.scalar.activation(out=win[t][:, :N], in_=h[t][:], func=COPY, scale=SIXTEENTH)
             fetch(g1[t], win[t], l_n1, t in ())
-        for t in range(PACK):
-            nc.vector.scalar_tensor_tensor(
-                out=win[t][:, :N], in0=h[t][:], scalar=SIXTEENTH, in1=g1[t][:], op0=ALU.mult, op1=ALU.subtract
-            )
-            pick("g1_%d" % t)
+            nc.gpsimd.tensor_tensor(out=win[t][:, :N], in0=win[t][:, :N], in1=g1[t][:], op=ALU.subtract)
         g2 = [new([P, N], F32, "g2_%d" % t) for t in range(PACK)]
         for t in range(PACK):
-            fetch(g2[t], win[t], l_n2, t in ())
+            fetch(g2[t], win[t], l_n2, t in (0,))
+        got["cand_w"] = deal(cand_gw, U32, "cand_w", "g1_3")
+        for t in range(PACK):
             nc.vector.tensor_tensor(out=win[t][:, :N], in0=win[t][:, :N], in1=g2[t][:], op=ALU.max)
-            pick("g2_%d" % t)
+            if t == 0:
+                got["cand_s"] = deal_bytes(cand_gs, "cand_s", "g2_0")
         z = new([P, PACK, N], F32, "z")
         g3 = [winb[t][:, :N] for t in range(PACK)]
         z_rounded = new([P, N, PACK], BF16, "z_rounded")
-        half_gain = new([P, PACK], F32, "half_gain")
-        nc.vector.tensor_scalar(out=half_gain[:], in0=gain[:], scalar1=0.5, scalar2=None, op0=ALU.mult)
         for t in range(PACK):
-            fetch(g3[t], win[t], l_n3, t in ())
+            fetch(g3[t], win[t], l_n3, t in (2,))
             nc.vector.tensor_scalar(
                 out=z[:, t, :], in0=win[t][:, :N], scalar1=gain[:, t : t + 1], scalar2=None, op0=ALU.mult
             )
@@ -221,14 +210,11 @@ def tile_picked_pqcjmaxbthree_none_po_kernel(
             )
 
         for t in range(PACK):
-            leave(t, winb[t], b[t], t in (3,))
-            if t < PACK - 1:
-                fetch(g5[t], winb[t], l_n5, False)
+            leave(t, winb[t], b[t], t in ())
+            fetch(g5[t], winb[t], l_n5, t in (3,))
         split = ()
         for t in range(PACK):
-            if t == 1:
-                fetch(g5[PACK - 1], winb[PACK - 1], l_n5, True)
-            leave(t, win[t], a[t], t in (0,))
+            leave(t, win[t], a[t], t in ())
             if t not in split:
                 fetch(g4[t], win[t], l_n4, t in (0,))
                 larger(t)

@@ -13,12 +13,16 @@ ALU = mybir.AluOpType
 COPY = mybir.ActivationFunctionType.Copy
 
 P = 128
-PACK = 4
+PLANES = 4
+FIRST, LAST = 0, PLANES - 1
 N = 512
 TOKENS = 1024
 CODEWORDS = 2048
-WIDE = 1024
-WIDE_ONE = 704
+SCALE_ROWS = 16
+LINE = 4
+WINDOW = 1024
+WINDOW_B = 704
+SCALAR_WEAVE = 160
 SIXTEENTH = 0.0625
 FLOPS = 3 * 2 * 512 * 512 * 512
 
@@ -27,213 +31,228 @@ def tile_picked_pqcjmaxbthree_none_po_kernel(
     tc, x_words, x_scales, d_words, d_scales, gs, offs, k1, n1, n2, n3, cand, two, k2, n4, n5, out_0, out_1, out_2
 ):
     nc = tc.nc
+    whole = slice(0, N)
+    halves = [slice(0, N // 2), slice(N // 2, N)]
+
     with ExitStack() as ctx:
         keep = ctx.enter_context(tc.tile_pool(name="keep", bufs=1))
         psum = ctx.enter_context(tc.psum_pool(name="psum", bufs=1))
 
-        def new(shape, dtype, name, tag=None):
-            return keep.tile(shape, dtype, name=name, tag=tag or name, align_bytes=64)
+        def new(shape, dtype, name, over=None):
+            return keep.tile(shape, dtype, name=name, tag=over or name, align_bytes=64)
 
         def load_list(src, name):
-            t = keep.tile([P, N // 16], U16, name=name)
-            nc.sync.dma_start(t[:], src)
-            return t
+            offsets = keep.tile([P, N // 16], U16, name=name)
+            nc.sync.dma_start(offsets[:], src)
+            return offsets
 
-        ds = new([P, CODEWORDS], U8, "ds")
-        xs = new([P, TOKENS], U8, "xs")
-        dw = new([P, CODEWORDS], U32, "dw")
-        xw = new([P, TOKENS], U32, "xw")
-        win = [new([P, WIDE], F32, "win%d" % t) for t in range(PACK)]
-        winb = [new([P, WIDE_ONE], F32, "winb%d" % t) for t in range(PACK)]
-        gain = new([P, PACK], F32, "gain")
-        nc.gpsimd.memset(ds[:].bitcast(I32), 0)
-        nc.vector.memset(xs[:].bitcast(I32), 0)
-        nc.scalar.dma_start(ds[0:P:8, :].bitcast(I32), d_scales[0].bitcast(I32))
-        l_k1 = load_list(k1, "l_k1")
-        nc.sync.dma_start(xw[:].bitcast(I32), x_words[0].rearrange("p n t -> p (n t)").bitcast(I32))
-        l_offs = load_list(offs, "l_offs")
-        for i in range(PACK):
-            if i == PACK - 1:
-                nc.sync.dma_start(dw[:].bitcast(I32), d_words[0].rearrange("p n t -> p (n t)").bitcast(I32))
-            nc.sync.dma_start(xs[i:P:32, :].bitcast(I32), x_scales[0][i:16:4, :].bitcast(I32))
-        l_n1 = load_list(n1, "l_n1")
-        l_n2 = load_list(n2, "l_n2")
-        l_n3 = load_list(n3, "l_n3")
-        l_k2 = load_list(k2, "l_k2")
-        l_two = load_list(two, "l_two")
-        l_cand = load_list(cand, "l_cand")
-        l_n5 = load_list(n5, "l_n5")
-        l_n4 = load_list(n4, "l_n4")
-        nc.sync.dma_start(gain[:], gs.rearrange("(p t) o -> p (t o)", t=PACK))
-        for t in range(PACK):
-            nc.vector.memset(win[t][:, N:], 0.0)
-            nc.vector.memset(winb[t][:, N:], 0.0)
+        def as_words(packed):
+            return packed[0].rearrange("p n t -> p (n t)").bitcast(I32)
 
-        def gather(table, lst, dtype, name, tag=None):
-            g = new([P, N], dtype, name, tag)
-            nc.vector.tensor_copy(out=g[:], in_=table[:].indirect(lst[:]))
-            return g
+        def pick(table, offsets, dtype, name):
+            picked = new([P, N], dtype, name)
+            nc.vector.tensor_copy(out=picked[:], in_=table[:].indirect(offsets[:]))
+            return picked
 
-        def deal(src, dtype, name, tag=None):
-            d = new([P, N], dtype, name, tag)
+        def deal_words(picked, name, over=None):
+            dealt = new([P, N], U32, name, over)
             nc.vector.tensor_copy(
-                out=d[:].rearrange("p (t c i) -> p c t i", t=PACK, i=4),
-                in_=src[:].rearrange("p (c i t) -> p c t i", t=PACK, i=4),
+                out=dealt[:].rearrange("p (t c i) -> p c t i", t=PLANES, i=LINE),
+                in_=picked[:].rearrange("p (c i t) -> p c t i", t=PLANES, i=LINE),
             )
-            return d
+            return dealt
 
-        def deal_bytes(src, name, tag=None):
-            d = new([P, N], U8, name, tag)
+        def deal_bytes(picked, name, over=None):
+            dealt = new([P, N], U8, name, over)
             nc.vector.tensor_copy(
-                out=d[:].rearrange("p (t m) -> p t m", t=PACK), in_=src[:].rearrange("p (m t) -> p t m", t=PACK)
+                out=dealt[:].rearrange("p (t m) -> p t m", t=PLANES),
+                in_=picked[:].rearrange("p (m t) -> p t m", t=PLANES),
             )
-            return d
+            return dealt
 
-        def code_scales(lst, name, queue, tag=None):
-            d = deal_bytes(gather(ds, lst, U8, name + "_gb", tag), name + "_db")
-            for i in range(1, PACK):
-                queue.dma_start(d[i:P:32, :].bitcast(I32), d[8 * i : P : 32, :].bitcast(I32))
-            return d
+        def pick_code_scales(offsets, name, queue):
+            dealt = deal_bytes(pick(d_scale_table, offsets, U8, name + "_picked"), name)
+            for i in range(1, PLANES):
+                queue.dma_start(dealt[i:P:32, :].bitcast(I32), dealt[8 * i : P : 32, :].bitcast(I32))
+            return dealt
 
-        def product(tag, lw, ls, rw, rs, width):
-            banks = [psum.tile([P, N], F32, name="%s%d" % (tag, t), tag="%s%d" % (tag, t)) for t in range(PACK)]
-            for t in range(PACK):
+        def product(banks_name, lhs_words, lhs_scales, rhs_words, rhs_scales):
+            names = ["%s%d" % (banks_name, t) for t in range(PLANES)]
+            banks = [psum.tile([P, N], F32, name=name, tag=name) for name in names]
+            for t in range(PLANES):
                 rows = slice(t * P, (t + 1) * P)
-                for c in range(0, N, width):
-                    cols = slice(c, c + width)
-                    nc.tensor.matmul_mx(
-                        out=banks[t][:, cols], lhsT=lw[:, rows].bitcast(FP8X4), lhsT_scale=ls[:, rows],
-                        rhs=rw[:, cols].bitcast(FP8X4), rhs_scale=rs[:, cols], start=True, stop=True,
-                    )
+                nc.tensor.matmul_mx(
+                    out=banks[t][:],
+                    lhsT=lhs_words[:, rows].bitcast(FP8X4),
+                    lhsT_scale=lhs_scales[:, rows],
+                    rhs=rhs_words[:].bitcast(FP8X4),
+                    rhs_scale=rhs_scales[:],
+                    start=True,
+                    stop=True,
+                )
             return banks
 
-        def fetch(out, window, lst, on_vector, lo=0, hi=N):
-            picked = window[:].indirect(lst[:, lo // 16 : hi // 16])
+        def leave_psum(window, bank, on_vector=False):
             if on_vector:
-                nc.vector.tensor_copy(out=out[:, lo:hi], in_=picked)
+                nc.vector.tensor_scalar(out=window[:, :N], in0=bank[:], scalar1=SIXTEENTH, scalar2=None, op0=ALU.mult)
             else:
-                nc.scalar.activation(out=out[:, lo:hi], in_=picked, func=COPY)
+                nc.scalar.activation(out=window[:, :N], in_=bank[:], func=COPY, scale=SIXTEENTH)
 
-        def weave(copy, rounded, src, cols):
+        def look_up(out, window, offsets, on_vector=False):
+            if on_vector:
+                nc.vector.tensor_copy(out=out, in_=window[:].indirect(offsets[:]))
+            else:
+                nc.scalar.activation(out=out, in_=window[:].indirect(offsets[:]), func=COPY)
+
+        def weave(copy, rounded, planes, cols):
             copy(
-                out=rounded[:, cols, :].rearrange("p (c i) t -> p c t i", i=4),
-                in_=src[:, :, cols].rearrange("p t (c i) -> p c t i", i=4),
+                out=rounded[:, cols, :].rearrange("p (c i) t -> p c t i", i=LINE),
+                in_=planes[:, :, cols].rearrange("p t (c i) -> p c t i", i=LINE),
             )
 
         def quantise(rounded, words, scales, cols):
             nc.vector.quantize_mx(
-                out=words[:, cols].bitcast(FP8X4), scales=scales[:, cols],
+                out=words[:, cols].bitcast(FP8X4),
+                scales=scales[:, cols],
                 in_=rounded[:, cols, :].rearrange("p c t -> p (c t)"),
             )
 
-        halves = [slice(0, N // 2), slice(N // 2, N)]
+        def parts(t):
+            return halves if t == LAST else [whole]
 
-        k1_s = code_scales(l_k1, "k1", nc.scalar)
-        offs_w = gather(xw, l_offs, U32, "offs_w")
-        offs_s = gather(xs, l_offs, U8, "offs_s")
-        k1_w = deal(gather(dw, l_k1, U32, "k1_gw"), U32, "k1_w")
-        h = product("h", k1_w, k1_s, offs_w, offs_s, N)
+        d_scale_table = new([P, CODEWORDS], U8, "d_scale_table")
+        x_scale_table = new([P, TOKENS], U8, "x_scale_table")
+        d_word_table = new([P, CODEWORDS], U32, "d_word_table")
+        x_word_table = new([P, TOKENS], U32, "x_word_table")
+        window = [new([P, WINDOW], F32, "window%d" % t) for t in range(PLANES)]
+        window_b = [new([P, WINDOW_B], F32, "window_b%d" % t) for t in range(PLANES)]
+        gain = new([P, PLANES], F32, "gain")
+        nc.gpsimd.memset(d_scale_table[:].bitcast(I32), 0)
+        nc.vector.memset(x_scale_table[:].bitcast(I32), 0)
+        nc.scalar.dma_start(d_scale_table[0:P:8, :].bitcast(I32), d_scales[0].bitcast(I32))
 
-        got = {}
-        got["k2_s"] = code_scales(l_k2, "k2", nc.sync)
-        got["k2_w"] = deal(gather(dw, l_k2, U32, "k2_gw"), U32, "k2_w")
-        got["two_w"] = gather(xw, l_two, U32, "two_w")
-        got["two_s"] = gather(xs, l_two, U8, "two_s")
-        cand_gw = gather(xw, l_cand, U32, "cand_gw")
-        cand_gs = gather(xs, l_cand, U8, "cand_gs")
-        half_gain = new([P, PACK], F32, "half_gain")
+        def load_x_scale_rows(i):
+            nc.sync.dma_start(x_scale_table[i:P:32, :].bitcast(I32), x_scales[0][i:SCALE_ROWS:PLANES, :].bitcast(I32))
+
+        k1_list = load_list(k1, "k1_list")
+        nc.sync.dma_start(x_word_table[:].bitcast(I32), as_words(x_words))
+        offs_list = load_list(offs, "offs_list")
+        for i in range(LAST):
+            load_x_scale_rows(i)
+        nc.sync.dma_start(d_word_table[:].bitcast(I32), as_words(d_words))
+        load_x_scale_rows(LAST)
+        n1_list = load_list(n1, "n1_list")
+        n2_list = load_list(n2, "n2_list")
+        n3_list = load_list(n3, "n3_list")
+        k2_list = load_list(k2, "k2_list")
+        two_list = load_list(two, "two_list")
+        cand_list = load_list(cand, "cand_list")
+        n5_list = load_list(n5, "n5_list")
+        n4_list = load_list(n4, "n4_list")
+        nc.sync.dma_start(gain[:], gs.rearrange("(p t) o -> p (t o)", t=PLANES))
+        for t in range(PLANES):
+            nc.vector.memset(window[t][:, N:], 0.0)
+            nc.vector.memset(window_b[t][:, N:], 0.0)
+
+        k1_scales = pick_code_scales(k1_list, "k1_scales", nc.scalar)
+        offs_words = pick(x_word_table, offs_list, U32, "offs_words")
+        offs_scales = pick(x_scale_table, offs_list, U8, "offs_scales")
+        k1_words = deal_words(pick(d_word_table, k1_list, U32, "k1_words_picked"), "k1_words")
+        h = product("ha", k1_words, k1_scales, offs_words, offs_scales)
+
+        k2_scales = pick_code_scales(k2_list, "k2_scales", nc.sync)
+        k2_words = deal_words(pick(d_word_table, k2_list, U32, "k2_words_picked"), "k2_words")
+        two_words = pick(x_word_table, two_list, U32, "two_words")
+        two_scales = pick(x_scale_table, two_list, U8, "two_scales")
+        cand_words_picked = pick(x_word_table, cand_list, U32, "cand_words_picked")
+        cand_scales_picked = pick(x_scale_table, cand_list, U8, "cand_scales_picked")
+        half_gain = new([P, PLANES], F32, "half_gain")
         nc.gpsimd.tensor_scalar(out=half_gain[:], in0=gain[:], scalar1=0.5, scalar2=0.0, op0=ALU.mult, op1=ALU.add)
-        g1 = [new([P, N], F32, "g1_%d" % t) for t in range(PACK)]
-        g1[2] = winb[0][:, :N]
-        for t in range(PACK):
-            nc.scalar.activation(out=win[t][:, :N], in_=h[t][:], func=COPY, scale=SIXTEENTH)
-            fetch(g1[t], win[t], l_n1, t in ())
-            nc.gpsimd.tensor_tensor(out=win[t][:, :N], in0=win[t][:, :N], in1=g1[t][:], op=ALU.subtract)
-        g2 = [new([P, N], F32, "g2_%d" % t) for t in range(PACK)]
-        for t in range(PACK):
-            fetch(g2[t], win[t], l_n2, t in (0,))
-        got["cand_w"] = deal(cand_gw, U32, "cand_w", "g1_3")
-        for t in range(PACK):
-            nc.vector.tensor_tensor(out=win[t][:, :N], in0=win[t][:, :N], in1=g2[t][:], op=ALU.max)
-            if t == 0:
-                got["cand_s"] = deal_bytes(cand_gs, "cand_s", "g2_0")
-        z = new([P, PACK, N], F32, "z")
-        g3 = [winb[t][:, :N] for t in range(PACK)]
-        z_rounded = new([P, N, PACK], BF16, "z_rounded")
-        for t in range(PACK):
-            fetch(g3[t], win[t], l_n3, t in (2,))
-            nc.vector.tensor_scalar(
-                out=z[:, t, :], in0=win[t][:, :N], scalar1=gain[:, t : t + 1], scalar2=None, op0=ALU.mult
+
+        su_n3 = [window_b[t][:, :N] for t in range(PLANES)]
+        h_n1 = [su_n3[FIRST] if t == LAST - 1 else new([P, N], F32, "h_n1_%d" % t)[:] for t in range(PLANES)]
+        for t in range(PLANES):
+            leave_psum(window[t], h[t])
+            look_up(h_n1[t], window[t], n1_list)
+            nc.gpsimd.tensor_tensor(out=window[t][:, :N], in0=window[t][:, :N], in1=h_n1[t], op=ALU.subtract)
+
+        st_n2 = [new([P, N], F32, "st_n2_%d" % t) for t in range(PLANES)]
+        for t in range(PLANES):
+            look_up(st_n2[t][:], window[t], n2_list, on_vector=t == FIRST)
+        cand_words = deal_words(cand_words_picked, "cand_words", over="h_n1_%d" % LAST)
+
+        def take_larger_st(t):
+            nc.vector.tensor_tensor(out=window[t][:, :N], in0=window[t][:, :N], in1=st_n2[t][:], op=ALU.max)
+
+        take_larger_st(FIRST)
+        cand_scales = deal_bytes(cand_scales_picked, "cand_scales", over="st_n2_%d" % FIRST)
+        for t in range(FIRST + 1, PLANES):
+            take_larger_st(t)
+
+        z = new([P, PLANES, N], F32, "z")
+        z_rounded = new([P, N, PLANES], BF16, "z_rounded")
+        for t in range(PLANES):
+            look_up(su_n3[t], window[t], n3_list, on_vector=t == LAST)
+            (nc.gpsimd if t == LAST else nc.vector).tensor_scalar(
+                out=z[:, t, :], in0=window[t][:, :N], scalar1=gain[:, t : t + 1], scalar2=0.0, op0=ALU.mult, op1=ALU.add
             )
-            for cols in halves if t == PACK - 1 else [slice(0, N)]:
+            for cols in parts(t):
                 nc.vector.scalar_tensor_tensor(
-                    out=z[:, t, cols], in0=g3[t][:, cols], scalar=half_gain[:, t : t + 1], in1=z[:, t, cols],
-                    op0=ALU.mult, op1=ALU.add,
+                    out=z[:, t, cols],
+                    in0=su_n3[t][:, cols],
+                    scalar=half_gain[:, t : t + 1],
+                    in1=z[:, t, cols],
+                    op0=ALU.mult,
+                    op1=ALU.add,
                 )
         for cols in halves:
             weave(nc.vector.tensor_copy, z_rounded, z, cols)
-        z_w = new([P, N], U32, "z_w")
-        z_s = new([P, N], U8, "z_s")
+        z_words = new([P, N], U32, "z_words")
+        z_scales = new([P, N], U8, "z_scales")
         for cols in halves:
-            quantise(z_rounded, z_w, z_s, cols)
+            quantise(z_rounded, z_words, z_scales, cols)
 
-        b = product("b", got["k2_w"], got["k2_s"], got["two_w"], got["two_s"], N)
-        a = product("h", got["cand_w"], got["cand_s"], z_w, z_s, N)
+        b = product("b", k2_words, k2_scales, two_words, two_scales)
+        a = product("ha", cand_words, cand_scales, z_words, z_scales)
 
-        y = new([P, PACK, N], F32, "y")
-        y_rounded = new([P, N, PACK], BF16, "y_rounded")
-        y_w = new([P, N], U32, "y_w")
-        y_s = new([P, N], U8, "y_s")
-        out_rows = out_0.rearrange("(p t) c -> p t c", t=PACK)
-        out_words = out_1[0].rearrange("p n t -> p (n t)").bitcast(I32)
-        g4 = [new([P, N], F32, "g4_%d" % t) for t in range(PACK)]
-        g5 = [new([P, N], F32, "g5_%d" % t) for t in range(PACK)]
-
-        def leave(t, dst, bank, on_vector):
-            if on_vector:
-                nc.vector.tensor_scalar(out=dst[:, :N], in0=bank[:], scalar1=SIXTEENTH, scalar2=None, op0=ALU.mult)
-            else:
-                nc.scalar.activation(out=dst[:, :N], in_=bank[:], func=COPY, scale=SIXTEENTH)
-
-        def smaller(t, cols):
+        y = new([P, PLANES, N], F32, "y")
+        y_rounded = new([P, N, PLANES], BF16, "y_rounded")
+        y_words = new([P, N], U32, "y_words")
+        y_scales = new([P, N], U8, "y_scales")
+        smaller = [new([P, N], F32, "smaller%d" % t) for t in range(PLANES)]
+        larger = [new([P, N], F32, "larger%d" % t) for t in range(PLANES)]
+        out_planes = out_0.rearrange("(p t) c -> p t c", t=PLANES)
+        for t in range(PLANES):
+            leave_psum(window_b[t], b[t], on_vector=t == LAST)
+            look_up(larger[t][:], window_b[t], n5_list, on_vector=t == LAST)
+        for t in range(PLANES):
+            leave_psum(window[t], a[t])
+            look_up(smaller[t][:], window[t], n4_list, on_vector=t == FIRST)
             nc.vector.scalar_tensor_tensor(
-                out=g4[t][:, cols], in0=b[t][:, cols], scalar=SIXTEENTH, in1=g4[t][:, cols], op0=ALU.mult, op1=ALU.min
+                out=larger[t][:], in0=a[t][:], scalar=SIXTEENTH, in1=larger[t][:], op0=ALU.mult, op1=ALU.max
             )
+            for cols in parts(t):
+                nc.vector.scalar_tensor_tensor(
+                    out=smaller[t][:, cols],
+                    in0=b[t][:, cols],
+                    scalar=SIXTEENTH,
+                    in1=smaller[t][:, cols],
+                    op0=ALU.mult,
+                    op1=ALU.min,
+                )
+            for cols in parts(t):
+                (nc.vector if t == LAST else nc.gpsimd).tensor_tensor(
+                    out=y[:, t, cols], in0=larger[t][:, cols], in1=smaller[t][:, cols], op=ALU.subtract
+                )
+            nc.sync.dma_start(out_planes[:, t, :], y[:, t, :])
 
-        def finish(t, cols):
-            eng = nc.gpsimd if t in (0,1,2) else nc.vector
-            eng.tensor_tensor(out=y[:, t, cols], in0=g5[t][:, cols], in1=g4[t][:, cols], op=ALU.subtract)
-
-        def larger(t):
-            nc.vector.scalar_tensor_tensor(
-                out=g5[t][:], in0=a[t][:], scalar=SIXTEENTH, in1=g5[t][:], op0=ALU.mult, op1=ALU.max
-            )
-
-        for t in range(PACK):
-            leave(t, winb[t], b[t], t in ())
-            fetch(g5[t], winb[t], l_n5, t in (3,))
-        split = ()
-        for t in range(PACK):
-            leave(t, win[t], a[t], t in ())
-            if t not in split:
-                fetch(g4[t], win[t], l_n4, t in (0,))
-                larger(t)
-                parts = halves if t == PACK - 1 else [slice(0, N)]
-                for cols in parts:
-                    smaller(t, cols)
-                for cols in parts:
-                    finish(t, cols)
-                nc.sync.dma_start(out_rows[:, t, :], y[:, t, :])
-        for c, cols in enumerate(halves):
-            for t in split:
-                fetch(g4[t], win[t], l_n4, False, cols.start, cols.stop)
-                finish(t, cols)
-                nc.sync.dma_start(out_rows[:, t, cols], y[:, t, cols])
-            cut = cols.stop - (0, 160)[c]
-            weave(nc.vector.tensor_copy, y_rounded, y, slice(cols.start, cut))
-            if cut < cols.stop:
-                weave(nc.scalar.copy, y_rounded, y, slice(cut, cols.stop))
-            quantise(y_rounded, y_w, y_s, cols)
-            nc.sync.dma_start(out_words[:, cols], y_w[:, cols].bitcast(I32))
-        for i in range(PACK):
-            nc.scalar.dma_start(out_2[0][i:16:4, :].bitcast(I32), y_s[i:P:32, :].bitcast(I32))
+        out_words = as_words(out_1)
+        weave(nc.vector.tensor_copy, y_rounded, y, halves[0])
+        quantise(y_rounded, y_words, y_scales, halves[0])
+        nc.sync.dma_start(out_words[:, halves[0]], y_words[:, halves[0]].bitcast(I32))
+        weave(nc.vector.tensor_copy, y_rounded, y, slice(N // 2, N - SCALAR_WEAVE))
+        weave(nc.scalar.copy, y_rounded, y, slice(N - SCALAR_WEAVE, N))
+        quantise(y_rounded, y_words, y_scales, halves[1])
+        nc.sync.dma_start(out_words[:, halves[1]], y_words[:, halves[1]].bitcast(I32))
+        for i in range(PLANES):
+            nc.scalar.dma_start(out_2[0][i:SCALE_ROWS:PLANES, :].bitcast(I32), y_scales[i:P:32, :].bitcast(I32))

from contextlib import ExitStack

import concourse.mybir as mybir

F32 = mybir.dt.float32
BF16 = mybir.dt.bfloat16
I32 = mybir.dt.int32
U32 = mybir.dt.uint32
U16 = mybir.dt.uint16
U8 = mybir.dt.uint8
FP8X4 = mybir.dt.float8_e4m3fn_x4
ALU = mybir.AluOpType
COPY = mybir.ActivationFunctionType.Copy

P = 128
PLANES = 4
FIRST, LAST = 0, PLANES - 1
N = 512
TOKENS = 1024
CODEWORDS = 2048
SCALE_ROWS = 16
LINE = 4
WINDOW = 1024
WINDOW_B = 704
SCALAR_WEAVE = 160
SIXTEENTH = 0.0625
FLOPS = 3 * 2 * 512 * 512 * 512


def tile_picked_pqcjmaxbthree_none_po_kernel(
    tc, x_words, x_scales, d_words, d_scales, gs, offs, k1, n1, n2, n3, cand, two, k2, n4, n5, out_0, out_1, out_2
):
    nc = tc.nc
    whole = slice(0, N)
    halves = [slice(0, N // 2), slice(N // 2, N)]

    with ExitStack() as ctx:
        keep = ctx.enter_context(tc.tile_pool(name="keep", bufs=1))
        psum = ctx.enter_context(tc.psum_pool(name="psum", bufs=1))

        def new(shape, dtype, name, over=None):
            return keep.tile(shape, dtype, name=name, tag=over or name, align_bytes=64)

        def load_list(src, name):
            offsets = keep.tile([P, N // 16], U16, name=name)
            nc.sync.dma_start(offsets[:], src)
            return offsets

        def as_words(packed):
            return packed[0].rearrange("p n t -> p (n t)").bitcast(I32)

        def pick(table, offsets, dtype, name):
            picked = new([P, N], dtype, name)
            nc.vector.tensor_copy(out=picked[:], in_=table[:].indirect(offsets[:]))
            return picked

        def deal_words(picked, name, over=None):
            dealt = new([P, N], U32, name, over)
            nc.vector.tensor_copy(
                out=dealt[:].rearrange("p (t c i) -> p c t i", t=PLANES, i=LINE),
                in_=picked[:].rearrange("p (c i t) -> p c t i", t=PLANES, i=LINE),
            )
            return dealt

        def deal_bytes(picked, name, over=None):
            dealt = new([P, N], U8, name, over)
            nc.vector.tensor_copy(
                out=dealt[:].rearrange("p (t m) -> p t m", t=PLANES),
                in_=picked[:].rearrange("p (m t) -> p t m", t=PLANES),
            )
            return dealt

        def pick_code_scales(offsets, name, queue):
            dealt = deal_bytes(pick(d_scale_table, offsets, U8, name + "_picked"), name)
            for i in range(1, PLANES):
                queue.dma_start(dealt[i:P:32, :].bitcast(I32), dealt[8 * i : P : 32, :].bitcast(I32))
            return dealt

        def product(banks_name, lhs_words, lhs_scales, rhs_words, rhs_scales):
            names = ["%s%d" % (banks_name, t) for t in range(PLANES)]
            banks = [psum.tile([P, N], F32, name=name, tag=name) for name in names]
            for t in range(PLANES):
                rows = slice(t * P, (t + 1) * P)
                nc.tensor.matmul_mx(
                    out=banks[t][:],
                    lhsT=lhs_words[:, rows].bitcast(FP8X4),
                    lhsT_scale=lhs_scales[:, rows],
                    rhs=rhs_words[:].bitcast(FP8X4),
                    rhs_scale=rhs_scales[:],
                    start=True,
                    stop=True,
                )
            return banks

        def leave_psum(window, bank, on_vector=False):
            if on_vector:
                nc.vector.tensor_scalar(out=window[:, :N], in0=bank[:], scalar1=SIXTEENTH, scalar2=None, op0=ALU.mult)
            else:
                nc.scalar.activation(out=window[:, :N], in_=bank[:], func=COPY, scale=SIXTEENTH)

        def look_up(out, window, offsets, on_vector=False):
            if on_vector:
                nc.vector.tensor_copy(out=out, in_=window[:].indirect(offsets[:]))
            else:
                nc.scalar.activation(out=out, in_=window[:].indirect(offsets[:]), func=COPY)

        def weave(copy, rounded, planes, cols):
            copy(
                out=rounded[:, cols, :].rearrange("p (c i) t -> p c t i", i=LINE),
                in_=planes[:, :, cols].rearrange("p t (c i) -> p c t i", i=LINE),
            )

        def quantise(rounded, words, scales, cols):
            nc.vector.quantize_mx(
                out=words[:, cols].bitcast(FP8X4),
                scales=scales[:, cols],
                in_=rounded[:, cols, :].rearrange("p c t -> p (c t)"),
            )

        def parts(t):
            return halves if t == LAST else [whole]

        d_scale_table = new([P, CODEWORDS], U8, "d_scale_table")
        x_scale_table = new([P, TOKENS], U8, "x_scale_table")
        d_word_table = new([P, CODEWORDS], U32, "d_word_table")
        x_word_table = new([P, TOKENS], U32, "x_word_table")
        window = [new([P, WINDOW], F32, "window%d" % t) for t in range(PLANES)]
        window_b = [new([P, WINDOW_B], F32, "window_b%d" % t) for t in range(PLANES)]
        gain = new([P, PLANES], F32, "gain")
        nc.gpsimd.memset(d_scale_table[:].bitcast(I32), 0)
        nc.vector.memset(x_scale_table[:].bitcast(I32), 0)
        nc.scalar.dma_start(d_scale_table[0:P:8, :].bitcast(I32), d_scales[0].bitcast(I32))

        def load_x_scale_rows(i):
            nc.sync.dma_start(x_scale_table[i:P:32, :].bitcast(I32), x_scales[0][i:SCALE_ROWS:PLANES, :].bitcast(I32))

        k1_list = load_list(k1, "k1_list")
        nc.sync.dma_start(x_word_table[:].bitcast(I32), as_words(x_words))
        offs_list = load_list(offs, "offs_list")
        for i in range(LAST):
            load_x_scale_rows(i)
        nc.sync.dma_start(d_word_table[:].bitcast(I32), as_words(d_words))
        load_x_scale_rows(LAST)
        n1_list = load_list(n1, "n1_list")
        n2_list = load_list(n2, "n2_list")
        n3_list = load_list(n3, "n3_list")
        k2_list = load_list(k2, "k2_list")
        two_list = load_list(two, "two_list")
        cand_list = load_list(cand, "cand_list")
        n5_list = load_list(n5, "n5_list")
        n4_list = load_list(n4, "n4_list")
        nc.sync.dma_start(gain[:], gs.rearrange("(p t) o -> p (t o)", t=PLANES))
        for t in range(PLANES):
            nc.vector.memset(window[t][:, N:], 0.0)
            nc.vector.memset(window_b[t][:, N:], 0.0)

        k1_scales = pick_code_scales(k1_list, "k1_scales", nc.scalar)
        offs_words = pick(x_word_table, offs_list, U32, "offs_words")
        offs_scales = pick(x_scale_table, offs_list, U8, "offs_scales")
        k1_words = deal_words(pick(d_word_table, k1_list, U32, "k1_words_picked"), "k1_words")
        h = product("ha", k1_words, k1_scales, offs_words, offs_scales)

        k2_scales = pick_code_scales(k2_list, "k2_scales", nc.sync)
        k2_words = deal_words(pick(d_word_table, k2_list, U32, "k2_words_picked"), "k2_words")
        two_words = pick(x_word_table, two_list, U32, "two_words")
        two_scales = pick(x_scale_table, two_list, U8, "two_scales")
        cand_words_picked = pick(x_word_table, cand_list, U32, "cand_words_picked")
        cand_scales_picked = pick(x_scale_table, cand_list, U8, "cand_scales_picked")
        half_gain = new([P, PLANES], F32, "half_gain")
        nc.gpsimd.tensor_scalar(out=half_gain[:], in0=gain[:], scalar1=0.5, scalar2=0.0, op0=ALU.mult, op1=ALU.add)

        su_n3 = [window_b[t][:, :N] for t in range(PLANES)]
        h_n1 = [su_n3[FIRST] if t == LAST - 1 else new([P, N], F32, "h_n1_%d" % t)[:] for t in range(PLANES)]
        for t in range(PLANES):
            leave_psum(window[t], h[t])
            look_up(h_n1[t], window[t], n1_list)
            nc.gpsimd.tensor_tensor(out=window[t][:, :N], in0=window[t][:, :N], in1=h_n1[t], op=ALU.subtract)

        st_n2 = [new([P, N], F32, "st_n2_%d" % t) for t in range(PLANES)]
        for t in range(PLANES):
            look_up(st_n2[t][:], window[t], n2_list, on_vector=t == FIRST)
        cand_words = deal_words(cand_words_picked, "cand_words", over="h_n1_%d" % LAST)

        def take_larger_st(t):
            nc.vector.tensor_tensor(out=window[t][:, :N], in0=window[t][:, :N], in1=st_n2[t][:], op=ALU.max)

        take_larger_st(FIRST)
        cand_scales = deal_bytes(cand_scales_picked, "cand_scales", over="st_n2_%d" % FIRST)
        for t in range(FIRST + 1, PLANES):
            take_larger_st(t)

        z = new([P, PLANES, N], F32, "z")
        z_rounded = new([P, N, PLANES], BF16, "z_rounded")
        for t in range(PLANES):
            look_up(su_n3[t], window[t], n3_list, on_vector=t == LAST)
            (nc.gpsimd if t == LAST else nc.vector).tensor_scalar(
                out=z[:, t, :], in0=window[t][:, :N], scalar1=gain[:, t : t + 1], scalar2=0.0, op0=ALU.mult, op1=ALU.add
            )
            for cols in parts(t):
                nc.vector.scalar_tensor_tensor(
                    out=z[:, t, cols],
                    in0=su_n3[t][:, cols],
                    scalar=half_gain[:, t : t + 1],
                    in1=z[:, t, cols],
                    op0=ALU.mult,
                    op1=ALU.add,
                )
        for cols in halves:
            weave(nc.vector.tensor_copy, z_rounded, z, cols)
        z_words = new([P, N], U32, "z_words")
        z_scales = new([P, N], U8, "z_scales")
        for cols in halves:
            quantise(z_rounded, z_words, z_scales, cols)

        b = product("b", k2_words, k2_scales, two_words, two_scales)
        a = product("ha", cand_words, cand_scales, z_words, z_scales)

        y = new([P, PLANES, N], F32, "y")
        y_rounded = new([P, N, PLANES], BF16, "y_rounded")
        y_words = new([P, N], U32, "y_words")
        y_scales = new([P, N], U8, "y_scales")
        smaller = [new([P, N], F32, "smaller%d" % t) for t in range(PLANES)]
        larger = [new([P, N], F32, "larger%d" % t) for t in range(PLANES)]
        out_planes = out_0.rearrange("(p t) c -> p t c", t=PLANES)
        for t in range(PLANES):
            leave_psum(window_b[t], b[t], on_vector=t == LAST)
            look_up(larger[t][:], window_b[t], n5_list, on_vector=t == LAST)
        for t in range(PLANES):
            leave_psum(window[t], a[t])
            look_up(smaller[t][:], window[t], n4_list, on_vector=t == FIRST)
            nc.vector.scalar_tensor_tensor(
                out=larger[t][:], in0=a[t][:], scalar=SIXTEENTH, in1=larger[t][:], op0=ALU.mult, op1=ALU.max
            )
            for cols in parts(t):
                nc.vector.scalar_tensor_tensor(
                    out=smaller[t][:, cols],
                    in0=b[t][:, cols],
                    scalar=SIXTEENTH,
                    in1=smaller[t][:, cols],
                    op0=ALU.mult,
                    op1=ALU.min,
                )
            for cols in parts(t):
                (nc.vector if t == LAST else nc.gpsimd).tensor_tensor(
                    out=y[:, t, cols], in0=larger[t][:, cols], in1=smaller[t][:, cols], op=ALU.subtract
                )
            nc.sync.dma_start(out_planes[:, t, :], y[:, t, :])

        out_words = as_words(out_1)
        weave(nc.vector.tensor_copy, y_rounded, y, halves[0])
        quantise(y_rounded, y_words, y_scales, halves[0])
        nc.sync.dma_start(out_words[:, halves[0]], y_words[:, halves[0]].bitcast(I32))
        weave(nc.vector.tensor_copy, y_rounded, y, slice(N // 2, N - SCALAR_WEAVE))
        weave(nc.scalar.copy, y_rounded, y, slice(N - SCALAR_WEAVE, N))
        quantise(y_rounded, y_words, y_scales, halves[1])
        nc.sync.dma_start(out_words[:, halves[1]], y_words[:, halves[1]].bitcast(I32))
        for i in range(PLANES):
            nc.scalar.dma_start(out_2[0][i:SCALE_ROWS:PLANES, :].bitcast(I32), y_scales[i:P:32, :].bitcast(I32))
